import numpy as np
import ml_dtypes


def mxq(x, axis, fmt="e4m3"):
    dtype, down = {"e4m3": (ml_dtypes.float8_e4m3fn, 7), "e5m2": (ml_dtypes.float8_e5m2, 14)}[fmt]
    v = np.moveaxis(np.asarray(x, np.float32).astype(ml_dtypes.bfloat16).astype(np.float64), axis, -1)
    blocks = v.reshape(v.shape[:-1] + (-1, 32))
    amax = np.abs(blocks).max(-1, keepdims=True)
    byte = np.maximum(np.where(amax > 0, np.frexp(amax)[1] - 1 + 127, 0) - down, 1)
    scale = np.exp2(byte - 127.0)
    codes = (blocks / scale).astype(np.float32).astype(dtype).astype(np.float64)
    return np.moveaxis((codes * scale).reshape(v.shape), -1, axis)


WIDE = False


def mx_kscale(k):
    if not WIDE:
        return np.ones(k)
    levels = np.array([10, -10, 5, -5, 0])
    if k % 512:
        return np.exp2(np.random.permutation(np.resize(levels, k // 32))).repeat(32)
    a = np.empty((k // 512, 16))
    for p in range(k // 512):
        a[p, :8] = np.random.permutation(np.resize(levels, 8))
        for g in range(8):
            far = levels[np.abs(levels - a[p, g]) >= 10]
            a[p, g + 8] = far[np.random.randint(len(far))]
    return np.exp2(a.ravel()).repeat(32)


def f64(x):
    return np.asarray(x).astype(np.float64)


def striped(idx):
    return np.tile(np.asarray(idx).reshape(-1, 16).T, (8, 1)).astype(np.uint16)


def unstriped(offs):
    return offs[:16].T.reshape(-1).astype(np.int64)


E2M1 = np.array([0.0, 0.5, 1.0, 1.5, 2.0, 3.0, 4.0, 6.0, -0.0, -0.5, -1.0, -1.5, -2.0, -3.0, -4.0, -6.0])


def pack_weight(w, fmt):
    k, n = w.shape
    w = f64(np.asarray(w, np.float32).astype(ml_dtypes.bfloat16)).reshape(k // 32, 32, n)
    amax = np.abs(w).max(1)
    if fmt == "e4m3":
        byte = np.frexp(amax)[1] - 1 + 127 - 7
    else:
        mant, ex = np.frexp(amax / 6.0)
        byte = np.where(mant > 0.5, ex, ex - 1) + 127
    byte = np.clip(np.where(amax > 0, byte, 1), 1, 254)
    scaled = (w * np.exp2(127.0 - byte)[:, None, :]).reshape(k, n).astype(np.float32)
    by_word = np.ascontiguousarray(scaled.reshape(k // 512, 128, 4, n).transpose(0, 1, 3, 2))
    if fmt == "e4m3":
        words = by_word.astype(ml_dtypes.float8_e4m3fn).view(np.uint8)
    else:
        c = by_word.astype(ml_dtypes.float4_e2m1fn).view(np.uint8) & 0xF
        words = (c[..., 0::2] | (c[..., 1::2] << 4)).reshape(k // 512, 128, 2 * n)
    return np.ascontiguousarray(words), np.ascontiguousarray(byte.astype(np.uint8).reshape(k // 512, 16, n))


def unpack_weight(words, scales, fmt):
    g, _, n = scales.shape
    words = np.ascontiguousarray(words).reshape(g, 128, n, -1)
    if fmt == "e4m3":
        vals = words.view(ml_dtypes.float8_e4m3fn).astype(np.float64)
    else:
        nib = np.empty((g, 128, n, 4), np.uint8)
        nib[..., 0::2] = words & 0xF
        nib[..., 1::2] = words >> 4
        vals = E2M1[nib]
    vals = vals * np.repeat(np.exp2(scales.astype(np.float64) - 127.0), 8, axis=1)[..., None]
    return vals.transpose(0, 1, 3, 2).reshape(g * 512, n)


D, T, I, Q, E, U, X = 512, 2048, 512, 128, 512, 1024, 1024


def setup_inputs():
    n = np.random.standard_normal
    idx = np.random.permutation(T)[:I]
    idx2 = np.random.permutation(U)[:Q]
    idx3 = np.random.permutation(U)[:Q]
    idx4 = np.random.permutation(X)[:I]
    fd = mx_kscale(D)
    fi = mx_kscale(I)
    keysp = pack_weight(n((D, T)) / fd[:, None], "e4m3")
    return {
        "users": (n((D, U)) * 1.0 / np.sqrt(D) * fd[:, None]).astype(np.float32),
        "keys_words": keysp[0],
        "keys_scales": keysp[1],
        "os": (np.random.uniform(0.02, 0.08, (1, I)) * fi).astype(np.float32),
        "vals": (n((E, T))).astype(np.float32),
        "vals2": (n((E, X))).astype(np.float32),
        "vsc": (np.random.uniform(0.5, 2.0, (1, I)) / fi).astype(np.float32),
        "offs": striped(idx),
        "offs2": striped(idx2),
        "offs3": striped(idx3),
        "offs4": striped(idx4),
    }


def reference(users, keys_words, keys_scales, os, vals, vals2, vsc, offs, offs2, offs3, offs4):
    idx = unstriped(offs)
    idx2 = unstriped(offs2)
    idx3 = unstriped(offs3)
    idx4 = unstriped(offs4)
    keysu = unpack_weight(keys_words, keys_scales, "e4m3")
    zq = np.maximum(f64(users)[:, idx2], f64(users)[:, idx3])
    zqq = mxq(zq, 0, "e4m3")
    keysidxg = keysu[:, idx]
    w = zqq.T @ keysidxg
    wo1 = w * f64(os)
    wt1 = wo1.T
    vz = np.maximum(f64(vals)[:, idx], f64(vals2)[:, idx4]) * f64(vsc)
    vt1 = vz.T
    wt1q = mxq(wt1, 0, "e4m3")
    vt1q = mxq(vt1, 0, "e4m3")
    o = wt1q.T @ vt1q
    return o

@@ -1,0 +1,176 @@
+from contextlib import ExitStack
+
+import concourse.mybir as mybir
+from concourse.masks import make_identity
+
+D, T, I, Q, E, U, X = 512, 2048, 512, 128, 512, 1024, 1024
+FLOPS = 2 * D * Q * I + 2 * I * Q * E
+
+F32 = mybir.dt.float32
+BF16 = mybir.dt.bfloat16
+I32 = mybir.dt.int32
+U32 = mybir.dt.uint32
+U16 = mybir.dt.uint16
+U8 = mybir.dt.uint8
+FP8X4 = mybir.dt.float8_e4m3fn_x4
+MAX = mybir.AluOpType.max
+MULT = mybir.AluOpType.mult
+COPY = mybir.ActivationFunctionType.Copy
+
+P = 128
+PACK = 4
+ROWS = 8
+BLOCKS = I // (PACK * ROWS)
+HALF = I // 2
+E_TILES = E // P
+
+
+def tile_attend_querylarger_mergedvalues_lean_kernel(
+    tc, users, keys_words, keys_scales, osc, vals, vals2, vsc, offs, offs2, offs3, offs4, out
+):
+    nc = tc.nc
+    with ExitStack() as ctx:
+        keep = ctx.enter_context(tc.tile_pool(name="keep", bufs=1))
+        psum = ctx.enter_context(tc.psum_pool(name="psum", bufs=1))
+
+        def sbuf(name, shape, dtype, buffer=None):
+            return keep.tile(shape, dtype, name=name, tag=buffer or name, align_bytes=64)
+
+        idx = sbuf("idx", [P, I // 16], U16)
+        idx2 = sbuf("idx2", [P, Q // 16], U16)
+        idx3 = sbuf("idx3", [P, Q // 16], U16)
+        idx4 = sbuf("idx4", [P, I // 16], U16)
+        key_words = sbuf("key_words", [P, T], I32)
+        key_bytes = sbuf("key_bytes", [P, T], U8)
+        user_pairs = [sbuf(f"users{h}", [P, 2, U], F32) for h in range(2)]
+        vals_rows = [sbuf(f"vals{j}", [P, T], F32) for j in range(E_TILES)]
+        vals2_rows = [sbuf(f"vals2_{j}", [P, X], F32) for j in range(E_TILES)]
+        factor_rows = sbuf("factor_rows", [P, P], F32)
+        identity = sbuf("identity", [P, P], F32)
+
+        nc.gpsimd.memset(factor_rows[:], 0.0)
+        nc.vector.memset(key_bytes[:].bitcast(I32), 0)
+        make_identity(nc, identity[:])
+        users_by_place = users.rearrange("(p t) u -> p t u", t=PACK)
+
+        def load_values(j):
+            nc.sync.dma_start(vals2_rows[j][:], vals2[j * P : (j + 1) * P, :])
+            nc.sync.dma_start(vals_rows[j][:], vals[j * P : (j + 1) * P, :])
+
+        nc.sync.dma_start(user_pairs[0][:], users_by_place[:, 0:2, :])
+        nc.sync.dma_start(idx2[:], offs2)
+        nc.sync.dma_start(idx3[:], offs3)
+        nc.sync.dma_start(user_pairs[1][:], users_by_place[:, 2:4, :])
+        nc.sync.dma_start(idx4[:], offs4)
+        nc.sync.dma_start(idx[:], offs)
+        load_values(0)
+        for quadrant in range(4):
+            nc.sync.dma_start(
+                key_bytes[32 * quadrant : 32 * quadrant + 4, :].bitcast(I32),
+                keys_scales[0, 4 * quadrant : 4 * quadrant + 4, :].bitcast(I32),
+            )
+        nc.sync.dma_start(key_words[:], keys_words[0].rearrange("p n t -> p (n t)").bitcast(I32))
+        for row, factor in ((0, osc), (PACK, vsc)):
+            nc.sync.dma_start(
+                factor_rows[row : row + PACK, :].rearrange("t (b r) -> t b r", r=ROWS),
+                factor[0].rearrange("(b t r) -> t b r", t=PACK, r=ROWS),
+            )
+        for j in range(1, E_TILES):
+            load_values(j)
+
+        def quantize(values, name, buffer=None):
+            codes = sbuf(name + "_codes", [P, P], U32, buffer)
+            scale_bytes = sbuf(name + "_bytes", [P, P], U8)
+            nc.vector.quantize_mx(codes[:].bitcast(FP8X4), scale_bytes[:], values[:].rearrange("p c t -> p (c t)"))
+            return codes[:], scale_bytes[:]
+
+        def multiply(sums, stationary, moving):
+            nc.tensor.matmul_mx(
+                sums,
+                lhsT=stationary[0].bitcast(FP8X4),
+                lhsT_scale=stationary[1],
+                rhs=moving[0].bitcast(FP8X4),
+                rhs_scale=moving[1],
+                start=True,
+                stop=True,
+            )
+
+        def merge_values(j, picked2_buffer, low_buffer):
+            picked2 = sbuf(f"picked2_{j}", [P, I], F32, picked2_buffer)
+            nc.scalar.activation(picked2[:], vals2_rows[j][:].indirect(idx4[:]), COPY)
+            low = sbuf(f"low{j}", [P, HALF], F32, low_buffer)
+            high = sbuf(f"high{j}", [P, HALF], F32, "high")
+            nc.vector.tensor_copy(low[:], vals_rows[j][:].indirect(idx[:, : HALF // 16]))
+            nc.scalar.activation(high[:], vals_rows[j][:].indirect(idx[:, HALF // 16 :]), COPY)
+            larger = sbuf(f"larger{j}", [P, PACK, BLOCKS, ROWS], F32)
+            for h, picked in enumerate((low, high)):
+                nc.vector.tensor_tensor(
+                    larger[:, :, h * BLOCKS // 2 : (h + 1) * BLOCKS // 2, :].rearrange("p t b r -> p b t r"),
+                    picked[:].rearrange("p (b t r) -> p b t r", t=PACK, r=ROWS),
+                    picked2[:, h * HALF : (h + 1) * HALF].rearrange("p (b t r) -> p b t r", t=PACK, r=ROWS),
+                    MAX,
+                )
+            turned = psum.tile([P, PACK, P], F32, name=f"turned{j}")
+            for t in range(PACK):
+                nc.tensor.transpose(turned[:, t, :], larger[:, t].rearrange("p b r -> p (b r)"), identity[:])
+            return turned
+
+        def scale_columns(name, sums, factor_cols, buffer=None):
+            scaled = sbuf(name, [P, P, PACK], BF16, buffer)
+            nc.vector.tensor_tensor(
+                scaled[:], sums[:].rearrange("p t c -> p c t"), factor_cols.unsqueeze(1).to_broadcast([P, P, PACK]), MULT
+            )
+            return scaled
+
+        first = sbuf("first", [P, PACK, Q], F32)
+        second = sbuf("second", [P, PACK, Q], F32)
+        for t in range(PACK):
+            plane = user_pairs[t // 2][:, t % 2, :]
+            nc.scalar.activation(first[:, t, :], plane.indirect(idx2[:]), COPY)
+            nc.vector.tensor_copy(second[:, t, :], plane.indirect(idx3[:]))
+        zq = sbuf("zq", [P, Q, PACK], BF16)
+        nc.vector.tensor_tensor(
+            zq[:], first[:].rearrange("p t q -> p q t"), second[:].rearrange("p t q -> p q t"), MAX
+        )
+        zq_mx = quantize(zq, "zq")
+
+        turned = merge_values(0, "users1", "zq")
+        slot_bytes = sbuf("slot_bytes", [P, PACK, BLOCKS, ROWS], U8, "users1")
+        nc.vector.tensor_copy(slot_bytes[:].rearrange("p t b r -> p b t r"), key_bytes[:].indirect(idx[:]))
+        slot_words = sbuf("slot_words", [P, PACK, BLOCKS, ROWS], U32, "high")
+        nc.vector.tensor_copy(
+            slot_words[:].rearrange("p t b r -> p b t r"), key_words[:].bitcast(U32).indirect(idx[:])
+        )
+        factor_ps = psum.tile([P, P], F32, name="factor_ps")
+        nc.tensor.transpose(factor_ps[:], factor_rows[:], identity[:])
+        factors = sbuf("factors", [P, 2 * PACK], F32, "key_words")
+        nc.vector.tensor_copy(factors[:], factor_ps[:, : 2 * PACK])
+        os_cols, vsc_cols = factors[:, :PACK], factors[:, PACK:]
+        scores = psum.tile([P, PACK, Q], F32, name="scores")
+        for t in range(PACK):
+            keys_t = [part[:, t].rearrange("p b r -> p (b r)") for part in (slot_words, slot_bytes)]
+            multiply(scores[:, t, :], keys_t, zq_mx)
+        vt = scale_columns("vt0", turned, vsc_cols)
+
+        last = E_TILES - 1
+        early_sums = psum.tile([P, last * P], F32, name="early_sums")
+        vt_mx = []
+        for j in range(1, E_TILES):
+            turned = merge_values(j, f"vals{j - 1}", f"larger{j - 1}")
+            vt_mx.append(quantize(vt, f"vt{j - 1}", f"vals{j - 1}"))
+            if j == 1:
+                wt = scale_columns("wt", scores, os_cols, "larger0")
+            if j == 2:
+                wt_mx = quantize(wt, "wt", "larger1")
+            vt = scale_columns(f"vt{j}", turned, vsc_cols)
+        for j in range(last):
+            multiply(early_sums[:, j * P : (j + 1) * P], wt_mx, vt_mx[j])
+        early_out = sbuf("early_out", [P, last * P], F32)
+        nc.scalar.copy(early_out[:], early_sums[:])
+        nc.sync.dma_start(out[:, : last * P], early_out[:])
+        last_mx = quantize(vt, f"vt{last}")
+        last_sums = psum.tile([P, P], F32, name="last_sums")
+        multiply(last_sums[:], wt_mx, last_mx)
+        last_out = sbuf("last_out", [P, P], F32)
+        nc.scalar.copy(last_out[:], last_sums[:])
+        nc.sync.dma_start(out[:, last * P :], last_out[:])

@@ -21,7 +21,8 @@ P = 128
 PACK = 4
 ROWS = 8
 BLOCKS = I // (PACK * ROWS)
-HALF = I // 2
+BLOCK = PACK * ROWS
+VECTOR_SLOTS = 256
 E_TILES = E // P
 
 
@@ -45,12 +46,13 @@ def tile_attend_querylarger_mergedvalues_lean_kernel(
         user_pairs = [sbuf(f"users{h}", [P, 2, U], F32) for h in range(2)]
         vals_rows = [sbuf(f"vals{j}", [P, T], F32) for j in range(E_TILES)]
         vals2_rows = [sbuf(f"vals2_{j}", [P, X], F32) for j in range(E_TILES)]
-        factor_rows = sbuf("factor_rows", [P, P], F32)
+        factor_rows = sbuf("factor_rows", [2, I], F32)
+        factor_dealt = sbuf("factor_dealt", [P, PACK, BLOCKS, ROWS], F32)
         identity = sbuf("identity", [P, P], F32)
 
-        nc.gpsimd.memset(factor_rows[:], 0.0)
         nc.vector.memset(key_bytes[:].bitcast(I32), 0)
         make_identity(nc, identity[:])
+        nc.gpsimd.memset(factor_dealt[:], 0.0)
         users_by_place = users.rearrange("(p t) u -> p t u", t=PACK)
 
         def load_values(j):
@@ -60,21 +62,16 @@ def tile_attend_querylarger_mergedvalues_lean_kernel(
         nc.sync.dma_start(user_pairs[0][:], users_by_place[:, 0:2, :])
         nc.sync.dma_start(idx2[:], offs2)
         nc.sync.dma_start(idx3[:], offs3)
+        nc.sync.dma_start(factor_rows[0:1, :], osc)
+        nc.sync.dma_start(factor_rows[1:2, :], vsc)
         nc.sync.dma_start(user_pairs[1][:], users_by_place[:, 2:4, :])
         nc.sync.dma_start(idx4[:], offs4)
+        nc.sync.dma_start(vals2_rows[0][:], vals2[:P, :])
         nc.sync.dma_start(idx[:], offs)
-        load_values(0)
-        for quadrant in range(4):
-            nc.sync.dma_start(
-                key_bytes[32 * quadrant : 32 * quadrant + 4, :].bitcast(I32),
-                keys_scales[0, 4 * quadrant : 4 * quadrant + 4, :].bitcast(I32),
-            )
+        nc.sync.dma_start(vals_rows[0][:], vals[:P, :])
+        for row in range(4):
+            nc.sync.dma_start(key_bytes[row:P:32, :].bitcast(I32), keys_scales[0, row:16:4, :].bitcast(I32))
         nc.sync.dma_start(key_words[:], keys_words[0].rearrange("p n t -> p (n t)").bitcast(I32))
-        for row, factor in ((0, osc), (PACK, vsc)):
-            nc.sync.dma_start(
-                factor_rows[row : row + PACK, :].rearrange("t (b r) -> t b r", r=ROWS),
-                factor[0].rearrange("(b t r) -> t b r", t=PACK, r=ROWS),
-            )
         for j in range(1, E_TILES):
             load_values(j)
 
@@ -95,19 +92,24 @@ def tile_attend_querylarger_mergedvalues_lean_kernel(
                 stop=True,
             )
 
-        def merge_values(j, picked2_buffer, low_buffer):
+        def merge_values(j, picked2_buffer, low_buffer=None):
             picked2 = sbuf(f"picked2_{j}", [P, I], F32, picked2_buffer)
             nc.scalar.activation(picked2[:], vals2_rows[j][:].indirect(idx4[:]), COPY)
-            low = sbuf(f"low{j}", [P, HALF], F32, low_buffer)
-            high = sbuf(f"high{j}", [P, HALF], F32, "high")
-            nc.vector.tensor_copy(low[:], vals_rows[j][:].indirect(idx[:, : HALF // 16]))
-            nc.scalar.activation(high[:], vals_rows[j][:].indirect(idx[:, HALF // 16 :]), COPY)
+            split = VECTOR_SLOTS if low_buffer else 0
+            parts = []
+            if split:
+                low = sbuf(f"low{j}", [P, split], F32, low_buffer)
+                nc.vector.tensor_copy(low[:], vals_rows[j][:].indirect(idx[:, : split // 16]))
+                parts.append((low, 0, split))
+            high = sbuf(f"high{j}", [P, I - split], F32, "high")
+            nc.scalar.activation(high[:], vals_rows[j][:].indirect(idx[:, split // 16 :]), COPY)
+            parts.append((high, split, I))
             larger = sbuf(f"larger{j}", [P, PACK, BLOCKS, ROWS], F32)
-            for h, picked in enumerate((low, high)):
+            for picked, begin, end in parts:
                 nc.vector.tensor_tensor(
-                    larger[:, :, h * BLOCKS // 2 : (h + 1) * BLOCKS // 2, :].rearrange("p t b r -> p b t r"),
+                    larger[:, :, begin // BLOCK : end // BLOCK, :].rearrange("p t b r -> p b t r"),
                     picked[:].rearrange("p (b t r) -> p b t r", t=PACK, r=ROWS),
-                    picked2[:, h * HALF : (h + 1) * HALF].rearrange("p (b t r) -> p b t r", t=PACK, r=ROWS),
+                    picked2[:, begin:end].rearrange("p (b t r) -> p b t r", t=PACK, r=ROWS),
                     MAX,
                 )
             turned = psum.tile([P, PACK, P], F32, name=f"turned{j}")
@@ -122,6 +124,16 @@ def tile_attend_querylarger_mergedvalues_lean_kernel(
             )
             return scaled
 
+        nc.vector.tensor_copy(
+            factor_dealt[0:2], factor_rows[:].rearrange("f (b t r) -> f t b r", t=PACK, r=ROWS)
+        )
+        factor_ps = psum.tile([P, PACK, P], F32, name="factor_ps", tag="bank_a")
+        for t in range(PACK):
+            nc.tensor.transpose(factor_ps[:, t, :], factor_dealt[:, t].rearrange("p b r -> p (b r)"), identity[:])
+        factors = sbuf("factors", [P, 2, PACK], F32)
+        nc.vector.tensor_copy(factors[:], factor_ps[:, :, 0:2].rearrange("p t f -> p f t"))
+        os_cols, vsc_cols = factors[:, 0, :], factors[:, 1, :]
+
         first = sbuf("first", [P, PACK, Q], F32)
         second = sbuf("second", [P, PACK, Q], F32)
         for t in range(PACK):
@@ -134,43 +146,37 @@ def tile_attend_querylarger_mergedvalues_lean_kernel(
         )
         zq_mx = quantize(zq, "zq")
 
-        turned = merge_values(0, "users1", "zq")
-        slot_bytes = sbuf("slot_bytes", [P, PACK, BLOCKS, ROWS], U8, "users1")
+        slot_bytes = sbuf("slot_bytes", [P, PACK, BLOCKS, ROWS], U8, "zq")
         nc.vector.tensor_copy(slot_bytes[:].rearrange("p t b r -> p b t r"), key_bytes[:].indirect(idx[:]))
-        slot_words = sbuf("slot_words", [P, PACK, BLOCKS, ROWS], U32, "high")
+        turned = merge_values(0, "users1")
+        slot_words = sbuf("slot_words", [P, PACK, BLOCKS, ROWS], U32, "users1")
         nc.vector.tensor_copy(
             slot_words[:].rearrange("p t b r -> p b t r"), key_words[:].bitcast(U32).indirect(idx[:])
         )
-        factor_ps = psum.tile([P, P], F32, name="factor_ps")
-        nc.tensor.transpose(factor_ps[:], factor_rows[:], identity[:])
-        factors = sbuf("factors", [P, 2 * PACK], F32, "key_words")
-        nc.vector.tensor_copy(factors[:], factor_ps[:, : 2 * PACK])
-        os_cols, vsc_cols = factors[:, :PACK], factors[:, PACK:]
         scores = psum.tile([P, PACK, Q], F32, name="scores")
         for t in range(PACK):
             keys_t = [part[:, t].rearrange("p b r -> p (b r)") for part in (slot_words, slot_bytes)]
             multiply(scores[:, t, :], keys_t, zq_mx)
-        vt = scale_columns("vt0", turned, vsc_cols)
+        vt_mx = [quantize(scale_columns("vt0", turned, vsc_cols, "key_words"), "vt0")]
 
-        last = E_TILES - 1
-        early_sums = psum.tile([P, last * P], F32, name="early_sums")
-        vt_mx = []
-        for j in range(1, E_TILES):
-            turned = merge_values(j, f"vals{j - 1}", f"larger{j - 1}")
-            vt_mx.append(quantize(vt, f"vt{j - 1}", f"vals{j - 1}"))
-            if j == 1:
-                wt = scale_columns("wt", scores, os_cols, "larger0")
-            if j == 2:
-                wt_mx = quantize(wt, "wt", "larger1")
-            vt = scale_columns(f"vt{j}", turned, vsc_cols)
-        for j in range(last):
+        turned1 = merge_values(1, "vals0", "key_words")
+        wt_mx = quantize(scale_columns("wt", scores, os_cols, "vals0"), "wt")
+        turned2 = merge_values(2, "vals1", "vals0")
+        vt_mx.append(quantize(scale_columns("vt1", turned1, vsc_cols, "vals1"), "vt1"))
+        early_sums = psum.tile([P, 2 * P], F32, name="early_sums")
+        for j in range(2):
             multiply(early_sums[:, j * P : (j + 1) * P], wt_mx, vt_mx[j])
-        early_out = sbuf("early_out", [P, last * P], F32)
+        turned3 = merge_values(3, "vals2", "vals1")
+        early_out = sbuf("early_out", [P, 2 * P], F32, "vals3")
         nc.scalar.copy(early_out[:], early_sums[:])
-        nc.sync.dma_start(out[:, : last * P], early_out[:])
-        last_mx = quantize(vt, f"vt{last}")
-        last_sums = psum.tile([P, P], F32, name="last_sums")
-        multiply(last_sums[:], wt_mx, last_mx)
-        last_out = sbuf("last_out", [P, P], F32)
-        nc.scalar.copy(last_out[:], last_sums[:])
-        nc.sync.dma_start(out[:, last * P :], last_out[:])
+        nc.sync.dma_start(out[:, : 2 * P], early_out[:])
+        vt2 = scale_columns("vt2", turned2, vsc_cols, "vals2")
+        vt3 = scale_columns("vt3", turned3, vsc_cols)
+        sums2 = psum.tile([P, P], F32, name="sums2", tag="bank_a")
+        multiply(sums2[:], wt_mx, quantize(vt2, "vt2"))
+        sums3 = psum.tile([P, P], F32, name="sums3")
+        multiply(sums3[:], wt_mx, quantize(vt3, "vt3"))
+        last_out = sbuf("last_out", [P, 2 * P], F32)
+        nc.scalar.copy(last_out[:, :P], sums2[:])
+        nc.vector.tensor_copy(last_out[:, P:], sums3[:])
+        nc.sync.dma_start(out[:, 2 * P :], last_out[:])

@@ -22,7 +22,8 @@ PACK = 4
 ROWS = 8
 BLOCKS = I // (PACK * ROWS)
 BLOCK = PACK * ROWS
-VECTOR_SLOTS = 256
+VECTOR_SLOTS = 352
+VECTOR_SLOTS_LAST = 288
 E_TILES = E // P
 
 
@@ -92,10 +93,9 @@ def tile_attend_querylarger_mergedvalues_lean_kernel(
                 stop=True,
             )
 
-        def merge_values(j, picked2_buffer, low_buffer=None):
+        def merge_values(j, split, picked2_buffer, low_buffer=None):
             picked2 = sbuf(f"picked2_{j}", [P, I], F32, picked2_buffer)
             nc.scalar.activation(picked2[:], vals2_rows[j][:].indirect(idx4[:]), COPY)
-            split = VECTOR_SLOTS if low_buffer else 0
             parts = []
             if split:
                 low = sbuf(f"low{j}", [P, split], F32, low_buffer)
@@ -148,7 +148,7 @@ def tile_attend_querylarger_mergedvalues_lean_kernel(
 
         slot_bytes = sbuf("slot_bytes", [P, PACK, BLOCKS, ROWS], U8, "zq")
         nc.vector.tensor_copy(slot_bytes[:].rearrange("p t b r -> p b t r"), key_bytes[:].indirect(idx[:]))
-        turned = merge_values(0, "users1")
+        turned = merge_values(0, 0, "users1")
         slot_words = sbuf("slot_words", [P, PACK, BLOCKS, ROWS], U32, "users1")
         nc.vector.tensor_copy(
             slot_words[:].rearrange("p t b r -> p b t r"), key_words[:].bitcast(U32).indirect(idx[:])
@@ -159,24 +159,21 @@ def tile_attend_querylarger_mergedvalues_lean_kernel(
             multiply(scores[:, t, :], keys_t, zq_mx)
         vt_mx = [quantize(scale_columns("vt0", turned, vsc_cols, "key_words"), "vt0")]
 
-        turned1 = merge_values(1, "vals0", "key_words")
+        turned1 = merge_values(1, VECTOR_SLOTS, "vals0", "key_words")
         wt_mx = quantize(scale_columns("wt", scores, os_cols, "vals0"), "wt")
-        turned2 = merge_values(2, "vals1", "vals0")
+        turned2 = merge_values(2, VECTOR_SLOTS, "vals1", "vals0")
         vt_mx.append(quantize(scale_columns("vt1", turned1, vsc_cols, "vals1"), "vt1"))
         early_sums = psum.tile([P, 2 * P], F32, name="early_sums")
         for j in range(2):
             multiply(early_sums[:, j * P : (j + 1) * P], wt_mx, vt_mx[j])
-        turned3 = merge_values(3, "vals2", "vals1")
+        turned3 = merge_values(3, VECTOR_SLOTS_LAST, "vals2", "vals1")
         early_out = sbuf("early_out", [P, 2 * P], F32, "vals3")
         nc.scalar.copy(early_out[:], early_sums[:])
         nc.sync.dma_start(out[:, : 2 * P], early_out[:])
-        vt2 = scale_columns("vt2", turned2, vsc_cols, "vals2")
-        vt3 = scale_columns("vt3", turned3, vsc_cols)
-        sums2 = psum.tile([P, P], F32, name="sums2", tag="bank_a")
-        multiply(sums2[:], wt_mx, quantize(vt2, "vt2"))
-        sums3 = psum.tile([P, P], F32, name="sums3")
-        multiply(sums3[:], wt_mx, quantize(vt3, "vt3"))
-        last_out = sbuf("last_out", [P, 2 * P], F32)
-        nc.scalar.copy(last_out[:, :P], sums2[:])
-        nc.vector.tensor_copy(last_out[:, P:], sums3[:])
-        nc.sync.dma_start(out[:, 2 * P :], last_out[:])
+        for j, turned, bank in ((2, turned2, "bank_a"), (3, turned3, "sums3")):
+            vt = scale_columns(f"vt{j}", turned, vsc_cols, "vals2")
+            sums = psum.tile([P, P], F32, name=f"sums{j}", tag=bank)
+            multiply(sums[:], wt_mx, quantize(vt, f"vt{j}"))
+            tile_out = sbuf(f"out{j}", [P, P], F32)
+            nc.scalar.copy(tile_out[:], sums[:])
+            nc.sync.dma_start(out[:, j * P : (j + 1) * P], tile_out[:])

from contextlib import ExitStack

import concourse.mybir as mybir
from concourse.masks import make_identity

D, T, I, Q, E, U, X = 512, 2048, 512, 128, 512, 1024, 1024
FLOPS = 2 * D * Q * I + 2 * I * Q * E

F32 = mybir.dt.float32
BF16 = mybir.dt.bfloat16
I32 = mybir.dt.int32
U32 = mybir.dt.uint32
U16 = mybir.dt.uint16
U8 = mybir.dt.uint8
FP8X4 = mybir.dt.float8_e4m3fn_x4
MAX = mybir.AluOpType.max
MULT = mybir.AluOpType.mult
COPY = mybir.ActivationFunctionType.Copy

P = 128
PACK = 4
ROWS = 8
BLOCKS = I // (PACK * ROWS)
BLOCK = PACK * ROWS
VECTOR_SLOTS = 352
VECTOR_SLOTS_LAST = 288
E_TILES = E // P


def tile_attend_querylarger_mergedvalues_lean_kernel(
    tc, users, keys_words, keys_scales, osc, vals, vals2, vsc, offs, offs2, offs3, offs4, out
):
    nc = tc.nc
    with ExitStack() as ctx:
        keep = ctx.enter_context(tc.tile_pool(name="keep", bufs=1))
        psum = ctx.enter_context(tc.psum_pool(name="psum", bufs=1))

        def sbuf(name, shape, dtype, buffer=None):
            return keep.tile(shape, dtype, name=name, tag=buffer or name, align_bytes=64)

        idx = sbuf("idx", [P, I // 16], U16)
        idx2 = sbuf("idx2", [P, Q // 16], U16)
        idx3 = sbuf("idx3", [P, Q // 16], U16)
        idx4 = sbuf("idx4", [P, I // 16], U16)
        key_words = sbuf("key_words", [P, T], I32)
        key_bytes = sbuf("key_bytes", [P, T], U8)
        user_pairs = [sbuf(f"users{h}", [P, 2, U], F32) for h in range(2)]
        vals_rows = [sbuf(f"vals{j}", [P, T], F32) for j in range(E_TILES)]
        vals2_rows = [sbuf(f"vals2_{j}", [P, X], F32) for j in range(E_TILES)]
        factor_rows = sbuf("factor_rows", [2, I], F32)
        factor_dealt = sbuf("factor_dealt", [P, PACK, BLOCKS, ROWS], F32)
        identity = sbuf("identity", [P, P], F32)

        nc.vector.memset(key_bytes[:].bitcast(I32), 0)
        make_identity(nc, identity[:])
        nc.gpsimd.memset(factor_dealt[:], 0.0)
        users_by_place = users.rearrange("(p t) u -> p t u", t=PACK)

        def load_values(j):
            nc.sync.dma_start(vals2_rows[j][:], vals2[j * P : (j + 1) * P, :])
            nc.sync.dma_start(vals_rows[j][:], vals[j * P : (j + 1) * P, :])

        nc.sync.dma_start(user_pairs[0][:], users_by_place[:, 0:2, :])
        nc.sync.dma_start(idx2[:], offs2)
        nc.sync.dma_start(idx3[:], offs3)
        nc.sync.dma_start(factor_rows[0:1, :], osc)
        nc.sync.dma_start(factor_rows[1:2, :], vsc)
        nc.sync.dma_start(user_pairs[1][:], users_by_place[:, 2:4, :])
        nc.sync.dma_start(idx4[:], offs4)
        nc.sync.dma_start(vals2_rows[0][:], vals2[:P, :])
        nc.sync.dma_start(idx[:], offs)
        nc.sync.dma_start(vals_rows[0][:], vals[:P, :])
        for row in range(4):
            nc.sync.dma_start(key_bytes[row:P:32, :].bitcast(I32), keys_scales[0, row:16:4, :].bitcast(I32))
        nc.sync.dma_start(key_words[:], keys_words[0].rearrange("p n t -> p (n t)").bitcast(I32))
        for j in range(1, E_TILES):
            load_values(j)

        def quantize(values, name, buffer=None):
            codes = sbuf(name + "_codes", [P, P], U32, buffer)
            scale_bytes = sbuf(name + "_bytes", [P, P], U8)
            nc.vector.quantize_mx(codes[:].bitcast(FP8X4), scale_bytes[:], values[:].rearrange("p c t -> p (c t)"))
            return codes[:], scale_bytes[:]

        def multiply(sums, stationary, moving):
            nc.tensor.matmul_mx(
                sums,
                lhsT=stationary[0].bitcast(FP8X4),
                lhsT_scale=stationary[1],
                rhs=moving[0].bitcast(FP8X4),
                rhs_scale=moving[1],
                start=True,
                stop=True,
            )

        def merge_values(j, split, picked2_buffer, low_buffer=None):
            picked2 = sbuf(f"picked2_{j}", [P, I], F32, picked2_buffer)
            nc.scalar.activation(picked2[:], vals2_rows[j][:].indirect(idx4[:]), COPY)
            parts = []
            if split:
                low = sbuf(f"low{j}", [P, split], F32, low_buffer)
                nc.vector.tensor_copy(low[:], vals_rows[j][:].indirect(idx[:, : split // 16]))
                parts.append((low, 0, split))
            high = sbuf(f"high{j}", [P, I - split], F32, "high")
            nc.scalar.activation(high[:], vals_rows[j][:].indirect(idx[:, split // 16 :]), COPY)
            parts.append((high, split, I))
            larger = sbuf(f"larger{j}", [P, PACK, BLOCKS, ROWS], F32)
            for picked, begin, end in parts:
                nc.vector.tensor_tensor(
                    larger[:, :, begin // BLOCK : end // BLOCK, :].rearrange("p t b r -> p b t r"),
                    picked[:].rearrange("p (b t r) -> p b t r", t=PACK, r=ROWS),
                    picked2[:, begin:end].rearrange("p (b t r) -> p b t r", t=PACK, r=ROWS),
                    MAX,
                )
            turned = psum.tile([P, PACK, P], F32, name=f"turned{j}")
            for t in range(PACK):
                nc.tensor.transpose(turned[:, t, :], larger[:, t].rearrange("p b r -> p (b r)"), identity[:])
            return turned

        def scale_columns(name, sums, factor_cols, buffer=None):
            scaled = sbuf(name, [P, P, PACK], BF16, buffer)
            nc.vector.tensor_tensor(
                scaled[:], sums[:].rearrange("p t c -> p c t"), factor_cols.unsqueeze(1).to_broadcast([P, P, PACK]), MULT
            )
            return scaled

        nc.vector.tensor_copy(
            factor_dealt[0:2], factor_rows[:].rearrange("f (b t r) -> f t b r", t=PACK, r=ROWS)
        )
        factor_ps = psum.tile([P, PACK, P], F32, name="factor_ps", tag="bank_a")
        for t in range(PACK):
            nc.tensor.transpose(factor_ps[:, t, :], factor_dealt[:, t].rearrange("p b r -> p (b r)"), identity[:])
        factors = sbuf("factors", [P, 2, PACK], F32)
        nc.vector.tensor_copy(factors[:], factor_ps[:, :, 0:2].rearrange("p t f -> p f t"))
        os_cols, vsc_cols = factors[:, 0, :], factors[:, 1, :]

        first = sbuf("first", [P, PACK, Q], F32)
        second = sbuf("second", [P, PACK, Q], F32)
        for t in range(PACK):
            plane = user_pairs[t // 2][:, t % 2, :]
            nc.scalar.activation(first[:, t, :], plane.indirect(idx2[:]), COPY)
            nc.vector.tensor_copy(second[:, t, :], plane.indirect(idx3[:]))
        zq = sbuf("zq", [P, Q, PACK], BF16)
        nc.vector.tensor_tensor(
            zq[:], first[:].rearrange("p t q -> p q t"), second[:].rearrange("p t q -> p q t"), MAX
        )
        zq_mx = quantize(zq, "zq")

        slot_bytes = sbuf("slot_bytes", [P, PACK, BLOCKS, ROWS], U8, "zq")
        nc.vector.tensor_copy(slot_bytes[:].rearrange("p t b r -> p b t r"), key_bytes[:].indirect(idx[:]))
        turned = merge_values(0, 0, "users1")
        slot_words = sbuf("slot_words", [P, PACK, BLOCKS, ROWS], U32, "users1")
        nc.vector.tensor_copy(
            slot_words[:].rearrange("p t b r -> p b t r"), key_words[:].bitcast(U32).indirect(idx[:])
        )
        scores = psum.tile([P, PACK, Q], F32, name="scores")
        for t in range(PACK):
            keys_t = [part[:, t].rearrange("p b r -> p (b r)") for part in (slot_words, slot_bytes)]
            multiply(scores[:, t, :], keys_t, zq_mx)
        vt_mx = [quantize(scale_columns("vt0", turned, vsc_cols, "key_words"), "vt0")]

        turned1 = merge_values(1, VECTOR_SLOTS, "vals0", "key_words")
        wt_mx = quantize(scale_columns("wt", scores, os_cols, "vals0"), "wt")
        turned2 = merge_values(2, VECTOR_SLOTS, "vals1", "vals0")
        vt_mx.append(quantize(scale_columns("vt1", turned1, vsc_cols, "vals1"), "vt1"))
        early_sums = psum.tile([P, 2 * P], F32, name="early_sums")
        for j in range(2):
            multiply(early_sums[:, j * P : (j + 1) * P], wt_mx, vt_mx[j])
        turned3 = merge_values(3, VECTOR_SLOTS_LAST, "vals2", "vals1")
        early_out = sbuf("early_out", [P, 2 * P], F32, "vals3")
        nc.scalar.copy(early_out[:], early_sums[:])
        nc.sync.dma_start(out[:, : 2 * P], early_out[:])
        for j, turned, bank in ((2, turned2, "bank_a"), (3, turned3, "sums3")):
            vt = scale_columns(f"vt{j}", turned, vsc_cols, "vals2")
            sums = psum.tile([P, P], F32, name=f"sums{j}", tag=bank)
            multiply(sums[:], wt_mx, quantize(vt, f"vt{j}"))
            tile_out = sbuf(f"out{j}", [P, P], F32)
            nc.scalar.copy(tile_out[:], sums[:])
            nc.sync.dma_start(out[:, j * P : (j + 1) * P], tile_out[:])
